import numpy as np
import ml_dtypes


def mxq(x, axis, fmt="e4m3"):
    dtype, down = {"e4m3": (ml_dtypes.float8_e4m3fn, 7), "e5m2": (ml_dtypes.float8_e5m2, 14)}[fmt]
    v = np.moveaxis(np.asarray(x, np.float32).astype(ml_dtypes.bfloat16).astype(np.float64), axis, -1)
    blocks = v.reshape(v.shape[:-1] + (-1, 32))
    amax = np.abs(blocks).max(-1, keepdims=True)
    byte = np.maximum(np.where(amax > 0, np.frexp(amax)[1] - 1 + 127, 0) - down, 1)
    scale = np.exp2(byte - 127.0)
    codes = (blocks / scale).astype(np.float32).astype(dtype).astype(np.float64)
    return np.moveaxis((codes * scale).reshape(v.shape), -1, axis)


WIDE = False


def mx_kscale(k):
    if not WIDE:
        return np.ones(k)
    levels = np.array([10, -10, 5, -5, 0])
    if k % 512:
        return np.exp2(np.random.permutation(np.resize(levels, k // 32))).repeat(32)
    a = np.empty((k // 512, 16))
    for p in range(k // 512):
        a[p, :8] = np.random.permutation(np.resize(levels, 8))
        for g in range(8):
            far = levels[np.abs(levels - a[p, g]) >= 10]
            a[p, g + 8] = far[np.random.randint(len(far))]
    return np.exp2(a.ravel()).repeat(32)


BF16 = ml_dtypes.bfloat16


def bf(x):
    return np.asarray(x, np.float32).astype(BF16)


def f64(x):
    return np.asarray(x).astype(np.float64)

def planes(Y):
    n, m = Y.shape
    b = f64(bf(Y)).reshape(n // 32, 32, m)
    amax = np.abs(b).max(1)
    byte = np.clip(np.where(amax > 0, np.frexp(amax)[1] - 1 + 127 - 7, 1), 1, 254)
    codes = (b * np.exp2(127.0 - byte)[:, None, :]).reshape(n, m).astype(np.float32).astype(ml_dtypes.float8_e4m3fn).view(np.uint8)
    words = codes.reshape(n // 512, 128, 4, m).transpose(0, 1, 3, 2)
    return np.ascontiguousarray(words), np.ascontiguousarray(byte.astype(np.uint8).reshape(n // 512, 16, m))


B, S, T, K, F = 4, 512, 512, 1024, 1024

def setup_inputs():
    rn = np.random.randn
    s = mx_kscale(K)
    t = mx_kscale(S)
    states = rn(B, S, K) * s
    w_hidden = 1.4 * rn(K, F) / np.sqrt(K) / s[:, None]
    state_weight = np.exp(0.3 * rn(B, S)) * t
    w_successor = rn(B, T, S) / np.sqrt(S) / t
    immediate = rn(B, T, F)
    discount = 0.7 + 0.25 * np.random.rand(B, T)
    feature_gain = np.exp(0.8 * rn(F))
    return {
        "states": bf(states),
        "w_hidden": bf(w_hidden),
        "state_weight": bf(state_weight),
        "w_successor": bf(w_successor),
        "immediate": bf(immediate),
        "discount": bf(discount),
        "feature_gain": bf(feature_gain),
    }

def reference(states, w_hidden, state_weight, w_successor, immediate, discount, feature_gain):
    x = f64(states).reshape(B * S, K)
    z = (mxq(x, 1, "e4m3") @ mxq(f64(w_hidden), 0, "e4m3")).reshape(B, S, F)
    h = np.maximum(z, 0.0) * f64(state_weight)[:, :, None]
    u = mxq(f64(w_successor), 2, "e4m3") @ mxq(h, 1, "e4m3")
    y = (f64(immediate) + f64(discount)[:, :, None] * u) * f64(feature_gain)
    Y = y.reshape(B * T, F).T
    words, scales = planes(Y)
    return y, words, scales

@@ -1,0 +1,399 @@
+from contextlib import ExitStack
+
+import concourse.mybir as mybir
+from concourse.masks import make_identity
+
+B, S, T, K, F = 4, 512, 512, 1024, 1024
+FLOPS = 2 * B * S * K * F + 2 * B * T * S * F
+
+F32 = mybir.dt.float32
+BF16 = mybir.dt.bfloat16
+I32 = mybir.dt.int32
+U32 = mybir.dt.uint32
+U8 = mybir.dt.uint8
+FP8X4 = mybir.dt.float8_e4m3fn_x4
+ALU = mybir.AluOpType
+
+P = 128
+PACK = 4
+PASS = 512
+UNITS = 8
+
+
+def tile_weighted_successor_features_h3_kernel(
+    tc, states, w_hidden, state_weight, w_successor, immediate, discount, feature_gain, out_0, out_1, out_2
+):
+    nc = tc.nc
+    words_out = out_1.rearrange("g p m t -> g p (m t)").bitcast(I32)
+    scales_out = out_2.bitcast(I32)
+
+    with ExitStack() as ctx:
+        sb = ctx.enter_context(tc.tile_pool(name="sb", bufs=1))
+        ps = ctx.enter_context(tc.psum_pool(name="ps", bufs=1))
+        ctx.enter_context(tc.manual_schedule())
+
+        def mx_bank():
+            return ps.tile([P, PASS], F32, name="mx_bank", tag="mx_bank", bufs=5)
+
+        def tr_bank():
+            return ps.tile([P, PASS], F32, name="tr_bank", tag="tr_bank", bufs=3)
+
+        def raw_tile():
+            return sb.tile([P, 2048], BF16, name="raw", tag="raw", bufs=20, align_bytes=64)
+
+        def packed_tile(tag):
+            return sb.tile([P, 2048], BF16, name=tag, tag=tag, bufs=2, align_bytes=64)
+
+        def quantize(tag, bufs, packed):
+            codes = sb.tile([P, PASS], U32, name=tag + "_codes", tag=tag + "_codes", bufs=bufs, align_bytes=64)
+            scales = sb.tile([P, PASS], U8, name=tag + "_scales", tag=tag + "_scales", bufs=bufs, align_bytes=64)
+            nc.vector.quantize_mx(out=codes[:].bitcast(FP8X4), scales=scales[:], in_=packed[:])
+            return codes, scales
+
+        x_raw, w_raw, ws_raw, imm = {}, {}, {}, {}
+        x_packed, w_packed, ws_packed, h_packed, y_packed = {}, {}, {}, {}, {}
+        xq, wq, wsq, hq = {}, {}, {}, {}
+        z_bank, u_bank, v, y, y16 = {}, {}, {}, {}, {}
+
+        def load_x(b, half):
+            x_raw[b, half] = raw_tile()
+            rows = states[b].rearrange("(m j) k -> m (j k)", j=PACK)
+            nc.sync.dma_start(out=x_raw[b, half][:], in_=rows[:, 2 * K * half : 2 * K * (half + 1)])
+
+        def load_w(kg, g):
+            w_raw[kg, g] = raw_tile()
+            rows = w_hidden[PASS * kg : PASS * (kg + 1), PASS * g : PASS * (g + 1)]
+            nc.sync.dma_start(
+                out=w_raw[kg, g][:].rearrange("p (j f) -> p j f", j=PACK),
+                in_=rows.rearrange("(p j) f -> p j f", j=PACK),
+            )
+
+        def load_ws(b):
+            ws_raw[b] = raw_tile()
+            nc.sync.dma_start(
+                out=ws_raw[b][:].rearrange("q (i s) -> q i s", i=4),
+                in_=w_successor[b].rearrange("(i q) s -> q i s", q=P),
+            )
+
+        def load_imm(n):
+            b, g = divmod(n, 2)
+            imm[n] = raw_tile()
+            nc.sync.dma_start(
+                out=imm[n][:].rearrange("q (i f) -> q i f", i=4),
+                in_=immediate[b][:, PASS * g : PASS * (g + 1)].rearrange("(i q) f -> q i f", q=P),
+            )
+
+        def turn_bank(sources, dest_words):
+            bank = tr_bank()
+            for c in range(4):
+                nc.tensor.transpose(bank[:, P * c : P * (c + 1)], sources[c], ident[:])
+            nc.scalar.copy(
+                out=dest_words.rearrange("p (a r u) -> p a r u", a=2, u=2),
+                in_=bank[:].rearrange("p (a u r) -> p a r u", a=2, u=2),
+            )
+
+        def turn_x(b, half):
+            x_packed[b, half] = packed_tile("x_packed")
+            words = x_raw[b, half][:].bitcast(F32)
+            dest = x_packed[b, half][:].bitcast(F32)
+            for j in range(2):
+                sources = [
+                    words[:, 512 * j + 256 * kg + u : 512 * j + 256 * (kg + 1) : 2] for kg in range(2) for u in range(2)
+                ]
+                turn_bank(sources, dest[:, 512 * j : 512 * (j + 1)])
+
+        def turn_ws(b, half):
+            if half == 0:
+                ws_packed[b] = packed_tile("ws_packed")
+            words = ws_raw[b][:].bitcast(F32)
+            dest = ws_packed[b][:].bitcast(F32)
+            sources = [
+                words[:, 256 * i + u : 256 * (i + 1) : 2] for i in (2 * half, 2 * half + 1) for u in range(2)
+            ]
+            turn_bank(sources, dest[:, 512 * half : 512 * (half + 1)])
+
+        def turn_y(n, half):
+            if half == 0:
+                y_packed[n] = packed_tile("y_packed")
+            dest = y_packed[n][:].bitcast(F32)
+            sources = [
+                y16[n, i].bitcast(F32)[:, P * u : P * (u + 1)] for i in (2 * half, 2 * half + 1) for u in range(2)
+            ]
+            turn_bank(sources, dest[:, 512 * half : 512 * (half + 1)])
+
+        def pack_w(kg, g, copy):
+            w_packed[kg, g] = packed_tile("w_packed")
+            copy(
+                out=w_packed[kg, g][:].rearrange("p (c i j) -> p c j i", i=4, j=PACK),
+                in_=w_raw[kg, g][:].rearrange("p (j c i) -> p c j i", i=4, j=PACK),
+            )
+
+        def matmul_z(n, c):
+            b, g = divmod(n, 2)
+            z_bank[n, c] = mx_bank()
+            cols = slice(P * c, P * (c + 1))
+            for j in range(PACK):
+                x_codes, x_scales = xq[b, j // 2]
+                for kg in range(2):
+                    w_codes, w_scales = wq[kg, g]
+                    rows = slice(P * (2 * (j % 2) + kg), P * (2 * (j % 2) + kg + 1))
+                    nc.tensor.matmul_mx(
+                        out=z_bank[n, c][:, P * j : P * (j + 1)],
+                        lhsT=x_codes[:, rows].bitcast(FP8X4),
+                        lhsT_scale=x_scales[:, rows],
+                        rhs=w_codes[:, cols].bitcast(FP8X4),
+                        rhs_scale=w_scales[:, cols],
+                        start=(kg == 0),
+                        stop=(kg == 1),
+                    )
+
+        def hidden(n, c):
+            b = n // 2
+            if c == 0:
+                h_packed[n] = packed_tile("h_packed")
+            nc.vector.scalar_tensor_tensor(
+                out=h_packed[n][:, PASS * c : PASS * (c + 1)].rearrange("p (f j) -> p f j", j=PACK),
+                in0=z_bank[n, c][:].rearrange("p (j f) -> p f j", j=PACK),
+                scalar=0.0,
+                in1=weight[:, PACK * b : PACK * (b + 1)].unsqueeze(1).to_broadcast([P, P, PACK]),
+                op0=ALU.max,
+                op1=ALU.mult,
+            )
+
+        def matmul_u(n, i):
+            ws_codes, ws_scales = wsq[n // 2]
+            h_codes, h_scales = hq[n]
+            u_bank[n, i] = mx_bank()
+            rows = slice(P * i, P * (i + 1))
+            nc.tensor.matmul_mx(
+                out=u_bank[n, i][:],
+                lhsT=ws_codes[:, rows].bitcast(FP8X4),
+                lhsT_scale=ws_scales[:, rows],
+                rhs=h_codes[:].bitcast(FP8X4),
+                rhs_scale=h_scales[:],
+                start=True,
+                stop=True,
+            )
+
+        def row_tiles(store, n, tag, dtype, bufs):
+            first = sb.tile([P, PASS], dtype, name=tag + "_first", tag=tag + "_first", bufs=bufs, align_bytes=64)
+            pair = sb.tile([P, 2 * PASS], dtype, name=tag + "_pair", tag=tag + "_pair", bufs=bufs, align_bytes=64)
+            last = sb.tile([P, PASS], dtype, name=tag + "_last", tag=tag + "_last", bufs=bufs, align_bytes=64)
+            store[n, 0] = first[:]
+            store[n, "pair"] = pair[:]
+            store[n, 1] = pair[:, :PASS]
+            store[n, 2] = pair[:, PASS:]
+            store[n, 3] = last[:]
+
+        def discount_add(n, i):
+            b = n // 2
+            if i == 0:
+                row_tiles(v, n, "v", F32, 2)
+                row_tiles(y, n, "y", F32, 4)
+                row_tiles(y16, n, "y16", BF16, 2)
+            nc.vector.scalar_tensor_tensor(
+                out=v[n, i],
+                in0=u_bank[n, i][:],
+                scalar=disc[:, 4 * b + i : 4 * b + i + 1],
+                in1=imm[n][:, PASS * i : PASS * (i + 1)],
+                op0=ALU.mult,
+                op1=ALU.add,
+            )
+
+        def apply_gain(engine, n, i):
+            b, g = divmod(n, 2)
+            gain_g = gain[:, PASS * g : PASS * (g + 1)]
+            cols = out_0[b][:, PASS * g : PASS * (g + 1)]
+            if i == "pair":
+                engine.tensor_tensor(
+                    out=y[n, i].rearrange("q (i f) -> q i f", i=2),
+                    in0=v[n, i].rearrange("q (i f) -> q i f", i=2),
+                    in1=gain_g.unsqueeze(1).to_broadcast([P, 2, PASS]),
+                    op=ALU.mult,
+                )
+                nc.sync.dma_start(
+                    out=cols[P : 3 * P, :].rearrange("(i q) f -> q i f", q=P),
+                    in_=y[n, i].rearrange("q (i f) -> q i f", i=2),
+                )
+            else:
+                engine.tensor_tensor(out=y[n, i], in0=v[n, i], in1=gain_g, op=ALU.mult)
+                nc.sync.dma_start(out=cols[P * i : P * (i + 1), :], in_=y[n, i])
+
+        def round_y(n, i):
+            tiles = 2 if i == "pair" else 1
+            nc.scalar.copy(
+                out=y16[n, i].rearrange("q (i u p e) -> q i u p e", i=tiles, u=2, e=2),
+                in_=y[n, i].rearrange("q (i p u e) -> q i u p e", i=tiles, u=2, e=2),
+            )
+
+        def quantize_y(n, halves):
+            b, g = divmod(n, 2)
+            width = T // halves
+            for half in range(halves):
+                codes = sb.tile([P, width], U32, name="y_codes", tag="y_codes", bufs=3, align_bytes=64)
+                if b < B - 1:
+                    plane = y_scales_a[:, 3 * T * g + T * b + width * half : 3 * T * g + T * b + width * (half + 1)]
+                else:
+                    plane = y_scales_b[:, T * g + width * half : T * g + width * (half + 1)]
+                nc.vector.quantize_mx(
+                    out=codes[:].bitcast(FP8X4),
+                    scales=plane,
+                    in_=y_packed[n][:, PACK * width * half : PACK * width * (half + 1)],
+                )
+                m0 = T * b + width * half
+                nc.sync.dma_start(out=words_out[g][:, m0 : m0 + width], in_=codes[:].bitcast(I32))
+
+        def store_scales(queue, plane, m0, width):
+            for q in range(4):
+                queue.dma_start(
+                    out=scales_out[:, 4 * q : 4 * q + 4, m0 // 4 : (m0 + width) // 4].rearrange("g r m -> r g m"),
+                    in_=plane[32 * q : 32 * q + 4, :].bitcast(I32).rearrange("r (g m) -> r g m", g=2),
+                )
+
+        ident = sb.tile([P, P], F32, name="ident")
+        weight = sb.tile([P, B * PACK], BF16, name="weight")
+        disc_rows16 = sb.tile([16, P], BF16, name="disc_rows16")
+        disc_rows = sb.tile([P, P], F32, name="disc_rows")
+        disc = sb.tile([P, 16], F32, name="disc")
+        gain_col16 = sb.tile([P, 8], BF16, name="gain_col16")
+        gain_col = sb.tile([P, 8], F32, name="gain_col")
+        gain = sb.tile([P, F], F32, name="gain")
+        y_scales_a = sb.tile([P, 2 * 3 * T], U8, name="y_scales_a", align_bytes=64)
+        y_scales_b = sb.tile([P, 2 * T], U8, name="y_scales_b", align_bytes=64)
+
+        load_x(0, 0)
+        load_x(0, 1)
+        load_w(0, 0)
+        load_w(1, 0)
+        nc.scalar.dma_start(
+            out=weight[:].rearrange("p (b j) -> p b j", j=PACK),
+            in_=state_weight.rearrange("b (p j) -> p b j", j=PACK),
+        )
+        nc.scalar.dma_start(out=disc_rows16[:], in_=discount.rearrange("b (i q) -> (b i) q", q=P))
+        nc.scalar.dma_start(out=gain_col16[:], in_=feature_gain.rearrange("(p c) -> p c", c=8))
+        load_ws(0)
+        load_w(0, 1)
+        load_w(1, 1)
+        load_imm(0)
+        load_x(1, 0)
+        load_ws(1)
+        load_x(1, 1)
+        load_imm(1)
+        for b in range(2, B):
+            load_x(b, 0)
+            load_imm(2 * b - 2)
+            load_ws(b)
+            load_x(b, 1)
+            if b == 2:
+                load_imm(2 * b - 1)
+
+        make_identity(nc, ident[:])
+        nc.gpsimd.memset(disc_rows[:], 0.0)
+        nc.vector.tensor_copy(out=disc_rows[0:16, :], in_=disc_rows16[:])
+        nc.vector.tensor_copy(out=gain_col[:], in_=gain_col16[:])
+
+        turn_x(0, 0)
+        turn_x(0, 1)
+        pack_w(0, 0, nc.vector.tensor_copy)
+        xq[0, 0] = quantize("x", 4, x_packed[0, 0])
+        wq[0, 0] = quantize("w", 4, w_packed[0, 0])
+        pack_w(1, 0, nc.vector.tensor_copy)
+        xq[0, 1] = quantize("x", 4, x_packed[0, 1])
+        wq[1, 0] = quantize("w", 4, w_packed[1, 0])
+
+        for n in range(5, UNITS):
+            load_imm(n)
+
+        bank = tr_bank()
+        nc.tensor.transpose(bank[:, :P], disc_rows[:], ident[:])
+        nc.scalar.copy(out=disc[:], in_=bank[:, :16])
+        pack_w(0, 1, nc.scalar.copy)
+        for c in range(4):
+            matmul_z(0, c)
+        turn_ws(0, 0)
+        turn_ws(0, 1)
+        for half in range(2):
+            bank = tr_bank()
+            for c in range(4):
+                column = gain_col[:, 4 * half + c : 4 * half + c + 1]
+                nc.tensor.transpose(bank[:, P * c : P * (c + 1)], column.to_broadcast([P, P]), ident[:])
+            nc.scalar.copy(
+                out=gain[:].rearrange("q (p c) -> q p c", c=8)[:, :, 4 * half : 4 * half + 4],
+                in_=bank[:].rearrange("q (c p) -> q p c", c=4),
+            )
+        for c in range(4):
+            hidden(0, c)
+        pack_w(1, 1, nc.vector.tensor_copy)
+        hq[0] = quantize("h", 2, h_packed[0])
+        wsq[0] = quantize("ws", 2, ws_packed[0])
+        for i in range(3):
+            matmul_u(0, i)
+        wq[0, 1] = quantize("w", 4, w_packed[0, 1])
+        wq[1, 1] = quantize("w", 4, w_packed[1, 1])
+
+        for n in range(1, UNITS):
+            nb, half = divmod(n + 2, 2)
+            if n == 1:
+                turn_x(1, 0)
+            elif nb < B:
+                turn_x(nb, half)
+            matmul_z(n, 0)
+            matmul_z(n, 1)
+            discount_add(n - 1, 0)
+            apply_gain(nc.gpsimd, n - 1, 0)
+            matmul_z(n, 2)
+            discount_add(n - 1, 1)
+            matmul_z(n, 3)
+            discount_add(n - 1, 2)
+            apply_gain(nc.gpsimd, n - 1, "pair")
+            round_y(n - 1, 0)
+            if n == 1:
+                turn_x(1, 1)
+            else:
+                turn_y(n - 2, 0)
+                turn_y(n - 2, 1)
+            matmul_u(n - 1, 3)
+            for c in range(4):
+                hidden(n, c)
+            discount_add(n - 1, 3)
+            round_y(n - 1, "pair")
+            if n == 1:
+                turn_ws(1, 0)
+                turn_ws(1, 1)
+            elif nb < B:
+                turn_ws(nb, half)
+            hq[n] = quantize("h", 2, h_packed[n])
+            for i in range(3):
+                matmul_u(n, i)
+            apply_gain(nc.vector, n - 1, 3)
+            round_y(n - 1, 3)
+            if n == 1:
+                xq[1, 0] = quantize("x", 4, x_packed[1, 0])
+                xq[1, 1] = quantize("x", 4, x_packed[1, 1])
+                wsq[1] = quantize("ws", 2, ws_packed[1])
+            else:
+                quantize_y(n - 2, 1)
+                if nb < B:
+                    xq[nb, half] = quantize("x", 4, x_packed[nb, half])
+                    if half == 1:
+                        wsq[nb] = quantize("ws", 2, ws_packed[nb])
+            if n == UNITS - 1:
+                store_scales(nc.sync, y_scales_a, 0, 3 * T)
+
+        n = UNITS - 1
+        matmul_u(n, 3)
+        turn_y(n - 1, 0)
+        turn_y(n - 1, 1)
+        discount_add(n, 0)
+        apply_gain(nc.gpsimd, n, 0)
+        for i in range(1, 4):
+            discount_add(n, i)
+        round_y(n, 0)
+        for i in range(1, 4):
+            apply_gain(nc.vector, n, i)
+            round_y(n, i)
+            if i % 2 == 1:
+                turn_y(n, i // 2)
+        quantize_y(n - 1, 1)
+        quantize_y(n, 2)
+        store_scales(nc.scalar, y_scales_b, 3 * T, T)

@@ -32,8 +32,8 @@ def tile_weighted_successor_features_h3_kernel(
         ps = ctx.enter_context(tc.psum_pool(name="ps", bufs=1))
         ctx.enter_context(tc.manual_schedule())
 
-        def mx_bank():
-            return ps.tile([P, PASS], F32, name="mx_bank", tag="mx_bank", bufs=5)
+        def mx_bank(index):
+            return ps.tile([P, PASS], F32, name="mx_bank", tag="mx_bank%d" % index, bufs=1)
 
         def tr_bank():
             return ps.tile([P, PASS], F32, name="tr_bank", tag="tr_bank", bufs=3)
@@ -41,19 +41,19 @@ def tile_weighted_successor_features_h3_kernel(
         def raw_tile():
             return sb.tile([P, 2048], BF16, name="raw", tag="raw", bufs=20, align_bytes=64)
 
-        def packed_tile(tag):
-            return sb.tile([P, 2048], BF16, name=tag, tag=tag, bufs=2, align_bytes=64)
+        def packed_tile(tag, bufs=2):
+            return sb.tile([P, 2048], BF16, name=tag, tag=tag, bufs=bufs, align_bytes=64)
 
-        def quantize(tag, bufs, packed):
-            codes = sb.tile([P, PASS], U32, name=tag + "_codes", tag=tag + "_codes", bufs=bufs, align_bytes=64)
-            scales = sb.tile([P, PASS], U8, name=tag + "_scales", tag=tag + "_scales", bufs=bufs, align_bytes=64)
+        def quantize(tag, bufs, packed, width=PASS):
+            codes = sb.tile([P, width], U32, name=tag + "_codes", tag=tag + "_codes", bufs=bufs, align_bytes=64)
+            scales = sb.tile([P, width], U8, name=tag + "_scales", tag=tag + "_scales", bufs=bufs, align_bytes=64)
             nc.vector.quantize_mx(out=codes[:].bitcast(FP8X4), scales=scales[:], in_=packed[:])
             return codes, scales
 
         x_raw, w_raw, ws_raw, imm = {}, {}, {}, {}
         x_packed, w_packed, ws_packed, h_packed, y_packed = {}, {}, {}, {}, {}
         xq, wq, wsq, hq = {}, {}, {}, {}
-        z_bank, u_bank, v, y, y16 = {}, {}, {}, {}, {}
+        z_bank, u_bank, v, y, y16, y_scales = {}, {}, {}, {}, {}, {}
 
         def load_x(b, half):
             x_raw[b, half] = raw_tile()
@@ -83,17 +83,17 @@ def tile_weighted_successor_features_h3_kernel(
                 in_=immediate[b][:, PASS * g : PASS * (g + 1)].rearrange("(i q) f -> q i f", q=P),
             )
 
-        def turn_bank(sources, dest_words):
+        def turn_bank(sources, dest_words, copy=nc.scalar.copy):
             bank = tr_bank()
-            for c in range(4):
+            for c in range(len(sources)):
                 nc.tensor.transpose(bank[:, P * c : P * (c + 1)], sources[c], ident[:])
-            nc.scalar.copy(
-                out=dest_words.rearrange("p (a r u) -> p a r u", a=2, u=2),
-                in_=bank[:].rearrange("p (a u r) -> p a r u", a=2, u=2),
+            copy(
+                out=dest_words.rearrange("p (a r u) -> p a r u", r=P, u=2),
+                in_=bank[:, : P * len(sources)].rearrange("p (a u r) -> p a r u", r=P, u=2),
             )
 
         def turn_x(b, half):
-            x_packed[b, half] = packed_tile("x_packed")
+            x_packed[b, half] = packed_tile("x_packed", 3)
             words = x_raw[b, half][:].bitcast(F32)
             dest = x_packed[b, half][:].bitcast(F32)
             for j in range(2):
@@ -102,40 +102,59 @@ def tile_weighted_successor_features_h3_kernel(
                 ]
                 turn_bank(sources, dest[:, 512 * j : 512 * (j + 1)])
 
-        def turn_ws(b, half):
-            if half == 0:
-                ws_packed[b] = packed_tile("ws_packed")
+        def turn_ws(b):
+            ws_packed[b] = packed_tile("ws_packed")
             words = ws_raw[b][:].bitcast(F32)
             dest = ws_packed[b][:].bitcast(F32)
-            sources = [
-                words[:, 256 * i + u : 256 * (i + 1) : 2] for i in (2 * half, 2 * half + 1) for u in range(2)
-            ]
-            turn_bank(sources, dest[:, 512 * half : 512 * (half + 1)])
+            for half in range(2):
+                sources = [
+                    words[:, 256 * i + u : 256 * (i + 1) : 2] for i in (2 * half, 2 * half + 1) for u in range(2)
+                ]
+                turn_bank(sources, dest[:, 512 * half : 512 * (half + 1)])
 
-        def turn_y(n, half):
-            if half == 0:
-                y_packed[n] = packed_tile("y_packed")
+        def turn_job(job):
+            if job[0] == "x":
+                turn_x(job[1], job[2])
+            elif job[0] == "ws":
+                turn_ws(job[1])
+            else:
+                turn_y(job[1], 0, 2)
+                turn_y(job[1], 2, 4)
+
+        def quantize_job(job):
+            if job[0] == "x":
+                xq[job[1], job[2]] = quantize("x", 4, x_packed[job[1], job[2]])
+            elif job[0] == "ws":
+                wsq[job[1]] = quantize("ws", 2, ws_packed[job[1]])
+            else:
+                quantize_y(job[1], 0, 4)
+
+        def turn_y(n, i0, i1, copy=nc.scalar.copy):
+            if i0 == 0:
+                y_packed[n] = packed_tile("y_packed", 3)
             dest = y_packed[n][:].bitcast(F32)
-            sources = [
-                y16[n, i].bitcast(F32)[:, P * u : P * (u + 1)] for i in (2 * half, 2 * half + 1) for u in range(2)
-            ]
-            turn_bank(sources, dest[:, 512 * half : 512 * (half + 1)])
+            sources = [y16[n, i].bitcast(F32)[:, P * u : P * (u + 1)] for i in range(i0, i1) for u in range(2)]
+            turn_bank(sources, dest[:, 256 * i0 : 256 * i1], copy)
 
-        def pack_w(kg, g, copy):
-            w_packed[kg, g] = packed_tile("w_packed")
+        def pack_w(kg, g, half, copy):
+            w_packed[kg, g, half] = sb.tile([P, 1024], BF16, name="w_packed", tag="w_packed", bufs=4, align_bytes=64)
+            cols = w_raw[kg, g][:].rearrange("p (j f) -> p j f", j=PACK)[:, :, 256 * half : 256 * (half + 1)]
             copy(
-                out=w_packed[kg, g][:].rearrange("p (c i j) -> p c j i", i=4, j=PACK),
-                in_=w_raw[kg, g][:].rearrange("p (j c i) -> p c j i", i=4, j=PACK),
+                out=w_packed[kg, g, half][:].rearrange("p (c i j) -> p c j i", i=4, j=PACK),
+                in_=cols.rearrange("p j (c i) -> p c j i", i=4),
             )
+
+        def quantize_w(kg, g, half):
+            wq[kg, g, half] = quantize("w", 8, w_packed[kg, g, half], 256)
 
         def matmul_z(n, c):
             b, g = divmod(n, 2)
-            z_bank[n, c] = mx_bank()
-            cols = slice(P * c, P * (c + 1))
+            z_bank[n, c] = mx_bank((4, 0, 1, 2)[c])
+            cols = slice(P * (c % 2), P * (c % 2 + 1))
             for j in range(PACK):
                 x_codes, x_scales = xq[b, j // 2]
                 for kg in range(2):
-                    w_codes, w_scales = wq[kg, g]
+                    w_codes, w_scales = wq[kg, g, c // 2]
                     rows = slice(P * (2 * (j % 2) + kg), P * (2 * (j % 2) + kg + 1))
                     nc.tensor.matmul_mx(
                         out=z_bank[n, c][:, P * j : P * (j + 1)],
@@ -163,7 +182,7 @@ def tile_weighted_successor_features_h3_kernel(
         def matmul_u(n, i):
             ws_codes, ws_scales = wsq[n // 2]
             h_codes, h_scales = hq[n]
-            u_bank[n, i] = mx_bank()
+            u_bank[n, i] = mx_bank(i)
             rows = slice(P * i, P * (i + 1))
             nc.tensor.matmul_mx(
                 out=u_bank[n, i][:],
@@ -219,35 +238,30 @@ def tile_weighted_successor_features_h3_kernel(
                 engine.tensor_tensor(out=y[n, i], in0=v[n, i], in1=gain_g, op=ALU.mult)
                 nc.sync.dma_start(out=cols[P * i : P * (i + 1), :], in_=y[n, i])
 
-        def round_y(n, i):
+        def round_y(n, i, copy=nc.scalar.copy):
             tiles = 2 if i == "pair" else 1
-            nc.scalar.copy(
+            copy(
                 out=y16[n, i].rearrange("q (i u p e) -> q i u p e", i=tiles, u=2, e=2),
                 in_=y[n, i].rearrange("q (i p u e) -> q i u p e", i=tiles, u=2, e=2),
             )
 
-        def quantize_y(n, halves):
+        def quantize_y(n, i0, i1):
             b, g = divmod(n, 2)
-            width = T // halves
-            for half in range(halves):
-                codes = sb.tile([P, width], U32, name="y_codes", tag="y_codes", bufs=3, align_bytes=64)
-                if b < B - 1:
-                    plane = y_scales_a[:, 3 * T * g + T * b + width * half : 3 * T * g + T * b + width * (half + 1)]
-                else:
-                    plane = y_scales_b[:, T * g + width * half : T * g + width * (half + 1)]
-                nc.vector.quantize_mx(
-                    out=codes[:].bitcast(FP8X4),
-                    scales=plane,
-                    in_=y_packed[n][:, PACK * width * half : PACK * width * (half + 1)],
-                )
-                m0 = T * b + width * half
-                nc.sync.dma_start(out=words_out[g][:, m0 : m0 + width], in_=codes[:].bitcast(I32))
+            if g == 0 and i0 == 0:
+                y_scales[b] = sb.tile([P, 2 * T], U8, name="y_scales", tag="y_scales", bufs=2, align_bytes=64)
+            codes = sb.tile([P, P * (i1 - i0)], U32, name="y_codes", tag="y_codes", bufs=4, align_bytes=64)
+            nc.vector.quantize_mx(
+                out=codes[:].bitcast(FP8X4),
+                scales=y_scales[b][:, T * g + P * i0 : T * g + P * i1],
+                in_=y_packed[n][:, PACK * P * i0 : PACK * P * i1],
+            )
+            nc.sync.dma_start(out=words_out[g][:, T * b + P * i0 : T * b + P * i1], in_=codes[:].bitcast(I32))
 
-        def store_scales(queue, plane, m0, width):
+        def store_scales(queue, b):
             for q in range(4):
                 queue.dma_start(
-                    out=scales_out[:, 4 * q : 4 * q + 4, m0 // 4 : (m0 + width) // 4].rearrange("g r m -> r g m"),
-                    in_=plane[32 * q : 32 * q + 4, :].bitcast(I32).rearrange("r (g m) -> r g m", g=2),
+                    out=scales_out[:, 4 * q : 4 * q + 4, T * b // 4 : T * (b + 1) // 4].rearrange("g r m -> r g m"),
+                    in_=y_scales[b][32 * q : 32 * q + 4, :].bitcast(I32).rearrange("r (g m) -> r g m", g=2),
                 )
 
         ident = sb.tile([P, P], F32, name="ident")
@@ -258,132 +272,129 @@ def tile_weighted_successor_features_h3_kernel(
         gain_col16 = sb.tile([P, 8], BF16, name="gain_col16")
         gain_col = sb.tile([P, 8], F32, name="gain_col")
         gain = sb.tile([P, F], F32, name="gain")
-        y_scales_a = sb.tile([P, 2 * 3 * T], U8, name="y_scales_a", align_bytes=64)
-        y_scales_b = sb.tile([P, 2 * T], U8, name="y_scales_b", align_bytes=64)
 
+        nc.scalar.dma_start(out=gain_col16[:], in_=feature_gain.rearrange("(p c) -> p c", c=8))
+        nc.scalar.dma_start(out=disc_rows16[:], in_=discount.rearrange("b (i q) -> (b i) q", q=P))
         load_x(0, 0)
-        load_x(0, 1)
         load_w(0, 0)
+        load_x(0, 1)
         load_w(1, 0)
-        nc.scalar.dma_start(
+        nc.sync.dma_start(
             out=weight[:].rearrange("p (b j) -> p b j", j=PACK),
             in_=state_weight.rearrange("b (p j) -> p b j", j=PACK),
         )
-        nc.scalar.dma_start(out=disc_rows16[:], in_=discount.rearrange("b (i q) -> (b i) q", q=P))
-        nc.scalar.dma_start(out=gain_col16[:], in_=feature_gain.rearrange("(p c) -> p c", c=8))
-        load_ws(0)
         load_w(0, 1)
         load_w(1, 1)
+        load_ws(0)
         load_imm(0)
         load_x(1, 0)
-        load_ws(1)
         load_x(1, 1)
+        load_ws(1)
         load_imm(1)
-        for b in range(2, B):
-            load_x(b, 0)
-            load_imm(2 * b - 2)
-            load_ws(b)
-            load_x(b, 1)
-            if b == 2:
-                load_imm(2 * b - 1)
+        load_x(2, 0)
+        load_x(2, 1)
+        load_imm(2)
+        load_ws(2)
+        load_x(3, 0)
+        load_imm(3)
+        load_x(3, 1)
+        load_ws(3)
 
         make_identity(nc, ident[:])
         nc.gpsimd.memset(disc_rows[:], 0.0)
-        nc.vector.tensor_copy(out=disc_rows[0:16, :], in_=disc_rows16[:])
-        nc.vector.tensor_copy(out=gain_col[:], in_=gain_col16[:])
+        nc.gpsimd.tensor_copy(out=gain_col[:], in_=gain_col16[:])
+        nc.gpsimd.tensor_copy(out=disc_rows[0:16, :], in_=disc_rows16[:])
 
-        turn_x(0, 0)
-        turn_x(0, 1)
-        pack_w(0, 0, nc.vector.tensor_copy)
-        xq[0, 0] = quantize("x", 4, x_packed[0, 0])
-        wq[0, 0] = quantize("w", 4, w_packed[0, 0])
-        pack_w(1, 0, nc.vector.tensor_copy)
-        xq[0, 1] = quantize("x", 4, x_packed[0, 1])
-        wq[1, 0] = quantize("w", 4, w_packed[1, 0])
-
-        for n in range(5, UNITS):
-            load_imm(n)
-
-        bank = tr_bank()
-        nc.tensor.transpose(bank[:, :P], disc_rows[:], ident[:])
-        nc.scalar.copy(out=disc[:], in_=bank[:, :16])
-        pack_w(0, 1, nc.scalar.copy)
-        for c in range(4):
-            matmul_z(0, c)
-        turn_ws(0, 0)
-        turn_ws(0, 1)
         for half in range(2):
             bank = tr_bank()
             for c in range(4):
                 column = gain_col[:, 4 * half + c : 4 * half + c + 1]
                 nc.tensor.transpose(bank[:, P * c : P * (c + 1)], column.to_broadcast([P, P]), ident[:])
-            nc.scalar.copy(
+            nc.vector.tensor_copy(
                 out=gain[:].rearrange("q (p c) -> q p c", c=8)[:, :, 4 * half : 4 * half + 4],
                 in_=bank[:].rearrange("q (c p) -> q p c", c=4),
             )
+        turn_x(0, 0)
+        pack_w(0, 0, 0, nc.vector.tensor_copy)
+        pack_w(0, 0, 1, nc.vector.tensor_copy)
+        quantize_w(0, 0, 0)
+        quantize_w(0, 0, 1)
+        xq[0, 0] = quantize("x", 4, x_packed[0, 0])
+        turn_x(0, 1)
+        bank = tr_bank()
+        nc.tensor.transpose(bank[:, :P], disc_rows[:], ident[:])
+        nc.scalar.copy(out=disc[:], in_=bank[:, :16])
+        pack_w(1, 0, 0, nc.vector.tensor_copy)
+        pack_w(1, 0, 1, nc.vector.tensor_copy)
+        quantize_w(1, 0, 0)
+        xq[0, 1] = quantize("x", 4, x_packed[0, 1])
+        quantize_w(1, 0, 1)
+
+        for n in range(4, UNITS):
+            load_imm(n)
+
+        pack_w(0, 1, 0, nc.scalar.copy)
+        pack_w(1, 1, 0, nc.scalar.copy)
+        pack_w(0, 1, 1, nc.scalar.copy)
+        pack_w(1, 1, 1, nc.scalar.copy)
+        for c in range(4):
+            matmul_z(0, c)
+        turn_ws(0)
         for c in range(4):
             hidden(0, c)
-        pack_w(1, 1, nc.vector.tensor_copy)
+        quantize_w(0, 1, 0)
         hq[0] = quantize("h", 2, h_packed[0])
+        quantize_w(1, 1, 0)
         wsq[0] = quantize("ws", 2, ws_packed[0])
-        for i in range(3):
+        matmul_z(1, 0)
+        for i in range(4):
             matmul_u(0, i)
-        wq[0, 1] = quantize("w", 4, w_packed[0, 1])
-        wq[1, 1] = quantize("w", 4, w_packed[1, 1])
+        quantize_w(0, 1, 1)
+        quantize_w(1, 1, 1)
 
+        slot_a = {1: [("x", 1, 0)], 2: [("ws", 1)], 3: [("x", 2, 1)], 4: [("ws", 2)], 5: [("x", 3, 1)], 6: [("ws", 3)], 7: [("y", 5)]}
+        slot_b = {1: [("x", 1, 1)], 2: [("y", 0)], 3: [("y", 1)], 4: [("y", 2)], 5: [("y", 3)], 6: [("y", 4)]}
+        slot_c = {2: [("x", 2, 0)], 4: [("x", 3, 0)]}
+        pre = {2: [("ws", 1)], 4: [("ws", 2)], 6: [("ws", 3)]}
+        post = {1: [("x", 1, 0), ("x", 1, 1)], 2: [("y", 0)], 3: [("x", 2, 0), ("x", 2, 1), ("y", 1)], 4: [("y", 2)], 5: [("x", 3, 0), ("x", 3, 1), ("y", 3)], 6: [("y", 4)], 7: [("y", 5)]}
+        late_z = (2,4,6)
         for n in range(1, UNITS):
-            nb, half = divmod(n + 2, 2)
-            if n == 1:
-                turn_x(1, 0)
-            elif nb < B:
-                turn_x(nb, half)
-            matmul_z(n, 0)
-            matmul_z(n, 1)
-            discount_add(n - 1, 0)
-            apply_gain(nc.gpsimd, n - 1, 0)
-            matmul_z(n, 2)
-            discount_add(n - 1, 1)
-            matmul_z(n, 3)
-            discount_add(n - 1, 2)
+            for job in slot_a.get(n, []):
+                turn_job(job)
+            for i in range(3):
+                discount_add(n - 1, i)
+                if i == 0:
+                    apply_gain(nc.gpsimd, n - 1, 0)
+                matmul_z(n, i + 1)
             apply_gain(nc.gpsimd, n - 1, "pair")
+            discount_add(n - 1, 3)
             round_y(n - 1, 0)
-            if n == 1:
-                turn_x(1, 1)
-            else:
-                turn_y(n - 2, 0)
-                turn_y(n - 2, 1)
-            matmul_u(n - 1, 3)
+            for job in slot_b.get(n, []):
+                turn_job(job)
             for c in range(4):
                 hidden(n, c)
-            discount_add(n - 1, 3)
+                if c == 0 and n + 1 < UNITS and n + 1 not in late_z:
+                    matmul_z(n + 1, 0)
+            for job in slot_c.get(n, []):
+                turn_job(job)
             round_y(n - 1, "pair")
-            if n == 1:
-                turn_ws(1, 0)
-                turn_ws(1, 1)
-            elif nb < B:
-                turn_ws(nb, half)
-            hq[n] = quantize("h", 2, h_packed[n])
-            for i in range(3):
-                matmul_u(n, i)
             apply_gain(nc.vector, n - 1, 3)
             round_y(n - 1, 3)
-            if n == 1:
-                xq[1, 0] = quantize("x", 4, x_packed[1, 0])
-                xq[1, 1] = quantize("x", 4, x_packed[1, 1])
-                wsq[1] = quantize("ws", 2, ws_packed[1])
-            else:
-                quantize_y(n - 2, 1)
-                if nb < B:
-                    xq[nb, half] = quantize("x", 4, x_packed[nb, half])
-                    if half == 1:
-                        wsq[nb] = quantize("ws", 2, ws_packed[nb])
-            if n == UNITS - 1:
-                store_scales(nc.sync, y_scales_a, 0, 3 * T)
+            for job in pre.get(n, []):
+                quantize_job(job)
+            hq[n] = quantize("h", 2, h_packed[n])
+            for i in range(4):
+                matmul_u(n, i)
+            for job in post.get(n, []):
+                quantize_job(job)
+                if job[0] == "y" and job[1] % 2 == 1:
+                    store_scales(nc.sync, job[1] // 2)
+            if n + 1 in late_z:
+                matmul_z(n + 1, 0)
 
         n = UNITS - 1
-        matmul_u(n, 3)
-        turn_y(n - 1, 0)
-        turn_y(n - 1, 1)
+        turn_y(n - 1, 0, 2)
+        turn_y(n - 1, 2, 4)
         discount_add(n, 0)
         apply_gain(nc.gpsimd, n, 0)
         for i in range(1, 4):
@@ -392,8 +403,11 @@ def tile_weighted_successor_features_h3_kernel(
         for i in range(1, 4):
             apply_gain(nc.vector, n, i)
             round_y(n, i)
-            if i % 2 == 1:
-                turn_y(n, i // 2)
-        quantize_y(n - 1, 1)
-        quantize_y(n, 2)
-        store_scales(nc.scalar, y_scales_b, 3 * T, T)
+        quantize_y(n - 1, 0, 4)
+        turn_y(n, 0, 2, nc.vector.tensor_copy)
+        turn_y(n, 2, 3)
+        turn_y(n, 3, 4)
+        quantize_y(n, 0, 2)
+        quantize_y(n, 2, 3)
+        quantize_y(n, 3, 4)
+        store_scales(nc.scalar, B - 1)

@@ -36,7 +36,7 @@ def tile_weighted_successor_features_h3_kernel(
             return ps.tile([P, PASS], F32, name="mx_bank", tag="mx_bank%d" % index, bufs=1)
 
         def tr_bank():
-            return ps.tile([P, PASS], F32, name="tr_bank", tag="tr_bank", bufs=3)
+            return ps.tile([P, PASS], F32, name="tr_bank", tag="tr_bank", bufs=2)
 
         def raw_tile():
             return sb.tile([P, 2048], BF16, name="raw", tag="raw", bufs=20, align_bytes=64)
@@ -219,9 +219,9 @@ def tile_weighted_successor_features_h3_kernel(
                 op1=ALU.add,
             )
 
-        def apply_gain(engine, n, i):
+        def apply_gain(engine, source, n, i):
             b, g = divmod(n, 2)
-            gain_g = gain[:, PASS * g : PASS * (g + 1)]
+            gain_g = source[:, PASS * g : PASS * (g + 1)]
             cols = out_0[b][:, PASS * g : PASS * (g + 1)]
             if i == "pair":
                 engine.tensor_tensor(
@@ -266,15 +266,16 @@ def tile_weighted_successor_features_h3_kernel(
 
         ident = sb.tile([P, P], F32, name="ident")
         weight = sb.tile([P, B * PACK], BF16, name="weight")
-        disc_rows16 = sb.tile([16, P], BF16, name="disc_rows16")
+        disc_rows16 = sb.tile([24, P], BF16, name="disc_rows16")
         disc_rows = sb.tile([P, P], F32, name="disc_rows")
         disc = sb.tile([P, 16], F32, name="disc")
-        gain_col16 = sb.tile([P, 8], BF16, name="gain_col16")
-        gain_col = sb.tile([P, 8], F32, name="gain_col")
+        ident16 = sb.tile([P, P], BF16, name="ident16")
+        gain_col = sb.tile([P, 8], BF16, name="gain_col")
+        gain_bank = ps.tile([P, F], BF16, name="gain_bank")
         gain = sb.tile([P, F], F32, name="gain")
 
-        nc.scalar.dma_start(out=gain_col16[:], in_=feature_gain.rearrange("(p c) -> p c", c=8))
-        nc.scalar.dma_start(out=disc_rows16[:], in_=discount.rearrange("b (i q) -> (b i) q", q=P))
+        nc.scalar.dma_start(out=disc_rows16[0:16, :], in_=discount.rearrange("b (i q) -> (b i) q", q=P))
+        nc.scalar.dma_start(out=disc_rows16[16:24, :], in_=feature_gain.rearrange("(c p) -> c p", p=P))
         load_x(0, 0)
         load_w(0, 0)
         load_x(0, 1)
@@ -302,18 +303,9 @@ def tile_weighted_successor_features_h3_kernel(
 
         make_identity(nc, ident[:])
         nc.gpsimd.memset(disc_rows[:], 0.0)
-        nc.gpsimd.tensor_copy(out=gain_col[:], in_=gain_col16[:])
-        nc.gpsimd.tensor_copy(out=disc_rows[0:16, :], in_=disc_rows16[:])
+        make_identity(nc, ident16[:])
+        nc.gpsimd.tensor_copy(out=disc_rows[0:24, :], in_=disc_rows16[:])
 
-        for half in range(2):
-            bank = tr_bank()
-            for c in range(4):
-                column = gain_col[:, 4 * half + c : 4 * half + c + 1]
-                nc.tensor.transpose(bank[:, P * c : P * (c + 1)], column.to_broadcast([P, P]), ident[:])
-            nc.vector.tensor_copy(
-                out=gain[:].rearrange("q (p c) -> q p c", c=8)[:, :, 4 * half : 4 * half + 4],
-                in_=bank[:].rearrange("q (c p) -> q p c", c=4),
-            )
         turn_x(0, 0)
         pack_w(0, 0, 0, nc.vector.tensor_copy)
         pack_w(0, 0, 1, nc.vector.tensor_copy)
@@ -324,6 +316,7 @@ def tile_weighted_successor_features_h3_kernel(
         bank = tr_bank()
         nc.tensor.transpose(bank[:, :P], disc_rows[:], ident[:])
         nc.scalar.copy(out=disc[:], in_=bank[:, :16])
+        nc.scalar.copy(out=gain_col[:], in_=bank[:, 16:24])
         pack_w(1, 0, 0, nc.vector.tensor_copy)
         pack_w(1, 0, 1, nc.vector.tensor_copy)
         quantize_w(1, 0, 0)
@@ -340,6 +333,10 @@ def tile_weighted_successor_features_h3_kernel(
         for c in range(4):
             matmul_z(0, c)
         turn_ws(0)
+        for c in range(8):
+            column = gain_col[:, c : c + 1]
+            nc.tensor.transpose(gain_bank[:, P * c : P * (c + 1)], column.to_broadcast([P, P]), ident16[:])
+        nc.scalar.copy(out=gain[:], in_=gain_bank[:])
         for c in range(4):
             hidden(0, c)
         quantize_w(0, 1, 0)
@@ -364,9 +361,9 @@ def tile_weighted_successor_features_h3_kernel(
             for i in range(3):
                 discount_add(n - 1, i)
                 if i == 0:
-                    apply_gain(nc.gpsimd, n - 1, 0)
+                    apply_gain(nc.gpsimd, gain, n - 1, 0)
                 matmul_z(n, i + 1)
-            apply_gain(nc.gpsimd, n - 1, "pair")
+            apply_gain(nc.gpsimd, gain, n - 1, "pair")
             discount_add(n - 1, 3)
             round_y(n - 1, 0)
             for job in slot_b.get(n, []):
@@ -378,7 +375,7 @@ def tile_weighted_successor_features_h3_kernel(
             for job in slot_c.get(n, []):
                 turn_job(job)
             round_y(n - 1, "pair")
-            apply_gain(nc.vector, n - 1, 3)
+            apply_gain(nc.vector, gain_bank, n - 1, 3)
             round_y(n - 1, 3)
             for job in pre.get(n, []):
                 quantize_job(job)
@@ -396,12 +393,12 @@ def tile_weighted_successor_features_h3_kernel(
         turn_y(n - 1, 0, 2)
         turn_y(n - 1, 2, 4)
         discount_add(n, 0)
-        apply_gain(nc.gpsimd, n, 0)
+        apply_gain(nc.gpsimd, gain, n, 0)
         for i in range(1, 4):
             discount_add(n, i)
         round_y(n, 0)
         for i in range(1, 4):
-            apply_gain(nc.vector, n, i)
+            apply_gain(nc.vector, gain_bank, n, i)
             round_y(n, i)
         quantize_y(n - 1, 0, 4)
         turn_y(n, 0, 2, nc.vector.tensor_copy)

from contextlib import ExitStack

import concourse.mybir as mybir
from concourse.masks import make_identity

B, S, T, K, F = 4, 512, 512, 1024, 1024
FLOPS = 2 * B * S * K * F + 2 * B * T * S * F

F32 = mybir.dt.float32
BF16 = mybir.dt.bfloat16
I32 = mybir.dt.int32
U32 = mybir.dt.uint32
U8 = mybir.dt.uint8
FP8X4 = mybir.dt.float8_e4m3fn_x4
ALU = mybir.AluOpType

P = 128
PACK = 4
PASS = 512
UNITS = 8


def tile_weighted_successor_features_h3_kernel(
    tc, states, w_hidden, state_weight, w_successor, immediate, discount, feature_gain, out_0, out_1, out_2
):
    nc = tc.nc
    words_out = out_1.rearrange("g p m t -> g p (m t)").bitcast(I32)
    scales_out = out_2.bitcast(I32)

    with ExitStack() as ctx:
        sb = ctx.enter_context(tc.tile_pool(name="sb", bufs=1))
        ps = ctx.enter_context(tc.psum_pool(name="ps", bufs=1))
        ctx.enter_context(tc.manual_schedule())

        def mx_bank(index):
            return ps.tile([P, PASS], F32, name="mx_bank", tag="mx_bank%d" % index, bufs=1)

        def tr_bank():
            return ps.tile([P, PASS], F32, name="tr_bank", tag="tr_bank", bufs=2)

        def raw_tile():
            return sb.tile([P, 2048], BF16, name="raw", tag="raw", bufs=20, align_bytes=64)

        def packed_tile(tag, bufs=2):
            return sb.tile([P, 2048], BF16, name=tag, tag=tag, bufs=bufs, align_bytes=64)

        def quantize(tag, bufs, packed, width=PASS):
            codes = sb.tile([P, width], U32, name=tag + "_codes", tag=tag + "_codes", bufs=bufs, align_bytes=64)
            scales = sb.tile([P, width], U8, name=tag + "_scales", tag=tag + "_scales", bufs=bufs, align_bytes=64)
            nc.vector.quantize_mx(out=codes[:].bitcast(FP8X4), scales=scales[:], in_=packed[:])
            return codes, scales

        x_raw, w_raw, ws_raw, imm = {}, {}, {}, {}
        x_packed, w_packed, ws_packed, h_packed, y_packed = {}, {}, {}, {}, {}
        xq, wq, wsq, hq = {}, {}, {}, {}
        z_bank, u_bank, v, y, y16, y_scales = {}, {}, {}, {}, {}, {}

        def load_x(b, half):
            x_raw[b, half] = raw_tile()
            rows = states[b].rearrange("(m j) k -> m (j k)", j=PACK)
            nc.sync.dma_start(out=x_raw[b, half][:], in_=rows[:, 2 * K * half : 2 * K * (half + 1)])

        def load_w(kg, g):
            w_raw[kg, g] = raw_tile()
            rows = w_hidden[PASS * kg : PASS * (kg + 1), PASS * g : PASS * (g + 1)]
            nc.sync.dma_start(
                out=w_raw[kg, g][:].rearrange("p (j f) -> p j f", j=PACK),
                in_=rows.rearrange("(p j) f -> p j f", j=PACK),
            )

        def load_ws(b):
            ws_raw[b] = raw_tile()
            nc.sync.dma_start(
                out=ws_raw[b][:].rearrange("q (i s) -> q i s", i=4),
                in_=w_successor[b].rearrange("(i q) s -> q i s", q=P),
            )

        def load_imm(n):
            b, g = divmod(n, 2)
            imm[n] = raw_tile()
            nc.sync.dma_start(
                out=imm[n][:].rearrange("q (i f) -> q i f", i=4),
                in_=immediate[b][:, PASS * g : PASS * (g + 1)].rearrange("(i q) f -> q i f", q=P),
            )

        def turn_bank(sources, dest_words, copy=nc.scalar.copy):
            bank = tr_bank()
            for c in range(len(sources)):
                nc.tensor.transpose(bank[:, P * c : P * (c + 1)], sources[c], ident[:])
            copy(
                out=dest_words.rearrange("p (a r u) -> p a r u", r=P, u=2),
                in_=bank[:, : P * len(sources)].rearrange("p (a u r) -> p a r u", r=P, u=2),
            )

        def turn_x(b, half):
            x_packed[b, half] = packed_tile("x_packed", 3)
            words = x_raw[b, half][:].bitcast(F32)
            dest = x_packed[b, half][:].bitcast(F32)
            for j in range(2):
                sources = [
                    words[:, 512 * j + 256 * kg + u : 512 * j + 256 * (kg + 1) : 2] for kg in range(2) for u in range(2)
                ]
                turn_bank(sources, dest[:, 512 * j : 512 * (j + 1)])

        def turn_ws(b):
            ws_packed[b] = packed_tile("ws_packed")
            words = ws_raw[b][:].bitcast(F32)
            dest = ws_packed[b][:].bitcast(F32)
            for half in range(2):
                sources = [
                    words[:, 256 * i + u : 256 * (i + 1) : 2] for i in (2 * half, 2 * half + 1) for u in range(2)
                ]
                turn_bank(sources, dest[:, 512 * half : 512 * (half + 1)])

        def turn_job(job):
            if job[0] == "x":
                turn_x(job[1], job[2])
            elif job[0] == "ws":
                turn_ws(job[1])
            else:
                turn_y(job[1], 0, 2)
                turn_y(job[1], 2, 4)

        def quantize_job(job):
            if job[0] == "x":
                xq[job[1], job[2]] = quantize("x", 4, x_packed[job[1], job[2]])
            elif job[0] == "ws":
                wsq[job[1]] = quantize("ws", 2, ws_packed[job[1]])
            else:
                quantize_y(job[1], 0, 4)

        def turn_y(n, i0, i1, copy=nc.scalar.copy):
            if i0 == 0:
                y_packed[n] = packed_tile("y_packed", 3)
            dest = y_packed[n][:].bitcast(F32)
            sources = [y16[n, i].bitcast(F32)[:, P * u : P * (u + 1)] for i in range(i0, i1) for u in range(2)]
            turn_bank(sources, dest[:, 256 * i0 : 256 * i1], copy)

        def pack_w(kg, g, half, copy):
            w_packed[kg, g, half] = sb.tile([P, 1024], BF16, name="w_packed", tag="w_packed", bufs=4, align_bytes=64)
            cols = w_raw[kg, g][:].rearrange("p (j f) -> p j f", j=PACK)[:, :, 256 * half : 256 * (half + 1)]
            copy(
                out=w_packed[kg, g, half][:].rearrange("p (c i j) -> p c j i", i=4, j=PACK),
                in_=cols.rearrange("p j (c i) -> p c j i", i=4),
            )

        def quantize_w(kg, g, half):
            wq[kg, g, half] = quantize("w", 8, w_packed[kg, g, half], 256)

        def matmul_z(n, c):
            b, g = divmod(n, 2)
            z_bank[n, c] = mx_bank((4, 0, 1, 2)[c])
            cols = slice(P * (c % 2), P * (c % 2 + 1))
            for j in range(PACK):
                x_codes, x_scales = xq[b, j // 2]
                for kg in range(2):
                    w_codes, w_scales = wq[kg, g, c // 2]
                    rows = slice(P * (2 * (j % 2) + kg), P * (2 * (j % 2) + kg + 1))
                    nc.tensor.matmul_mx(
                        out=z_bank[n, c][:, P * j : P * (j + 1)],
                        lhsT=x_codes[:, rows].bitcast(FP8X4),
                        lhsT_scale=x_scales[:, rows],
                        rhs=w_codes[:, cols].bitcast(FP8X4),
                        rhs_scale=w_scales[:, cols],
                        start=(kg == 0),
                        stop=(kg == 1),
                    )

        def hidden(n, c):
            b = n // 2
            if c == 0:
                h_packed[n] = packed_tile("h_packed")
            nc.vector.scalar_tensor_tensor(
                out=h_packed[n][:, PASS * c : PASS * (c + 1)].rearrange("p (f j) -> p f j", j=PACK),
                in0=z_bank[n, c][:].rearrange("p (j f) -> p f j", j=PACK),
                scalar=0.0,
                in1=weight[:, PACK * b : PACK * (b + 1)].unsqueeze(1).to_broadcast([P, P, PACK]),
                op0=ALU.max,
                op1=ALU.mult,
            )

        def matmul_u(n, i):
            ws_codes, ws_scales = wsq[n // 2]
            h_codes, h_scales = hq[n]
            u_bank[n, i] = mx_bank(i)
            rows = slice(P * i, P * (i + 1))
            nc.tensor.matmul_mx(
                out=u_bank[n, i][:],
                lhsT=ws_codes[:, rows].bitcast(FP8X4),
                lhsT_scale=ws_scales[:, rows],
                rhs=h_codes[:].bitcast(FP8X4),
                rhs_scale=h_scales[:],
                start=True,
                stop=True,
            )

        def row_tiles(store, n, tag, dtype, bufs):
            first = sb.tile([P, PASS], dtype, name=tag + "_first", tag=tag + "_first", bufs=bufs, align_bytes=64)
            pair = sb.tile([P, 2 * PASS], dtype, name=tag + "_pair", tag=tag + "_pair", bufs=bufs, align_bytes=64)
            last = sb.tile([P, PASS], dtype, name=tag + "_last", tag=tag + "_last", bufs=bufs, align_bytes=64)
            store[n, 0] = first[:]
            store[n, "pair"] = pair[:]
            store[n, 1] = pair[:, :PASS]
            store[n, 2] = pair[:, PASS:]
            store[n, 3] = last[:]

        def discount_add(n, i):
            b = n // 2
            if i == 0:
                row_tiles(v, n, "v", F32, 2)
                row_tiles(y, n, "y", F32, 4)
                row_tiles(y16, n, "y16", BF16, 2)
            nc.vector.scalar_tensor_tensor(
                out=v[n, i],
                in0=u_bank[n, i][:],
                scalar=disc[:, 4 * b + i : 4 * b + i + 1],
                in1=imm[n][:, PASS * i : PASS * (i + 1)],
                op0=ALU.mult,
                op1=ALU.add,
            )

        def apply_gain(engine, source, n, i):
            b, g = divmod(n, 2)
            gain_g = source[:, PASS * g : PASS * (g + 1)]
            cols = out_0[b][:, PASS * g : PASS * (g + 1)]
            if i == "pair":
                engine.tensor_tensor(
                    out=y[n, i].rearrange("q (i f) -> q i f", i=2),
                    in0=v[n, i].rearrange("q (i f) -> q i f", i=2),
                    in1=gain_g.unsqueeze(1).to_broadcast([P, 2, PASS]),
                    op=ALU.mult,
                )
                nc.sync.dma_start(
                    out=cols[P : 3 * P, :].rearrange("(i q) f -> q i f", q=P),
                    in_=y[n, i].rearrange("q (i f) -> q i f", i=2),
                )
            else:
                engine.tensor_tensor(out=y[n, i], in0=v[n, i], in1=gain_g, op=ALU.mult)
                nc.sync.dma_start(out=cols[P * i : P * (i + 1), :], in_=y[n, i])

        def round_y(n, i, copy=nc.scalar.copy):
            tiles = 2 if i == "pair" else 1
            copy(
                out=y16[n, i].rearrange("q (i u p e) -> q i u p e", i=tiles, u=2, e=2),
                in_=y[n, i].rearrange("q (i p u e) -> q i u p e", i=tiles, u=2, e=2),
            )

        def quantize_y(n, i0, i1):
            b, g = divmod(n, 2)
            if g == 0 and i0 == 0:
                y_scales[b] = sb.tile([P, 2 * T], U8, name="y_scales", tag="y_scales", bufs=2, align_bytes=64)
            codes = sb.tile([P, P * (i1 - i0)], U32, name="y_codes", tag="y_codes", bufs=4, align_bytes=64)
            nc.vector.quantize_mx(
                out=codes[:].bitcast(FP8X4),
                scales=y_scales[b][:, T * g + P * i0 : T * g + P * i1],
                in_=y_packed[n][:, PACK * P * i0 : PACK * P * i1],
            )
            nc.sync.dma_start(out=words_out[g][:, T * b + P * i0 : T * b + P * i1], in_=codes[:].bitcast(I32))

        def store_scales(queue, b):
            for q in range(4):
                queue.dma_start(
                    out=scales_out[:, 4 * q : 4 * q + 4, T * b // 4 : T * (b + 1) // 4].rearrange("g r m -> r g m"),
                    in_=y_scales[b][32 * q : 32 * q + 4, :].bitcast(I32).rearrange("r (g m) -> r g m", g=2),
                )

        ident = sb.tile([P, P], F32, name="ident")
        weight = sb.tile([P, B * PACK], BF16, name="weight")
        disc_rows16 = sb.tile([24, P], BF16, name="disc_rows16")
        disc_rows = sb.tile([P, P], F32, name="disc_rows")
        disc = sb.tile([P, 16], F32, name="disc")
        ident16 = sb.tile([P, P], BF16, name="ident16")
        gain_col = sb.tile([P, 8], BF16, name="gain_col")
        gain_bank = ps.tile([P, F], BF16, name="gain_bank")
        gain = sb.tile([P, F], F32, name="gain")

        nc.scalar.dma_start(out=disc_rows16[0:16, :], in_=discount.rearrange("b (i q) -> (b i) q", q=P))
        nc.scalar.dma_start(out=disc_rows16[16:24, :], in_=feature_gain.rearrange("(c p) -> c p", p=P))
        load_x(0, 0)
        load_w(0, 0)
        load_x(0, 1)
        load_w(1, 0)
        nc.sync.dma_start(
            out=weight[:].rearrange("p (b j) -> p b j", j=PACK),
            in_=state_weight.rearrange("b (p j) -> p b j", j=PACK),
        )
        load_w(0, 1)
        load_w(1, 1)
        load_ws(0)
        load_imm(0)
        load_x(1, 0)
        load_x(1, 1)
        load_ws(1)
        load_imm(1)
        load_x(2, 0)
        load_x(2, 1)
        load_imm(2)
        load_ws(2)
        load_x(3, 0)
        load_imm(3)
        load_x(3, 1)
        load_ws(3)

        make_identity(nc, ident[:])
        nc.gpsimd.memset(disc_rows[:], 0.0)
        make_identity(nc, ident16[:])
        nc.gpsimd.tensor_copy(out=disc_rows[0:24, :], in_=disc_rows16[:])

        turn_x(0, 0)
        pack_w(0, 0, 0, nc.vector.tensor_copy)
        pack_w(0, 0, 1, nc.vector.tensor_copy)
        quantize_w(0, 0, 0)
        quantize_w(0, 0, 1)
        xq[0, 0] = quantize("x", 4, x_packed[0, 0])
        turn_x(0, 1)
        bank = tr_bank()
        nc.tensor.transpose(bank[:, :P], disc_rows[:], ident[:])
        nc.scalar.copy(out=disc[:], in_=bank[:, :16])
        nc.scalar.copy(out=gain_col[:], in_=bank[:, 16:24])
        pack_w(1, 0, 0, nc.vector.tensor_copy)
        pack_w(1, 0, 1, nc.vector.tensor_copy)
        quantize_w(1, 0, 0)
        xq[0, 1] = quantize("x", 4, x_packed[0, 1])
        quantize_w(1, 0, 1)

        for n in range(4, UNITS):
            load_imm(n)

        pack_w(0, 1, 0, nc.scalar.copy)
        pack_w(1, 1, 0, nc.scalar.copy)
        pack_w(0, 1, 1, nc.scalar.copy)
        pack_w(1, 1, 1, nc.scalar.copy)
        for c in range(4):
            matmul_z(0, c)
        turn_ws(0)
        for c in range(8):
            column = gain_col[:, c : c + 1]
            nc.tensor.transpose(gain_bank[:, P * c : P * (c + 1)], column.to_broadcast([P, P]), ident16[:])
        nc.scalar.copy(out=gain[:], in_=gain_bank[:])
        for c in range(4):
            hidden(0, c)
        quantize_w(0, 1, 0)
        hq[0] = quantize("h", 2, h_packed[0])
        quantize_w(1, 1, 0)
        wsq[0] = quantize("ws", 2, ws_packed[0])
        matmul_z(1, 0)
        for i in range(4):
            matmul_u(0, i)
        quantize_w(0, 1, 1)
        quantize_w(1, 1, 1)

        slot_a = {1: [("x", 1, 0)], 2: [("ws", 1)], 3: [("x", 2, 1)], 4: [("ws", 2)], 5: [("x", 3, 1)], 6: [("ws", 3)], 7: [("y", 5)]}
        slot_b = {1: [("x", 1, 1)], 2: [("y", 0)], 3: [("y", 1)], 4: [("y", 2)], 5: [("y", 3)], 6: [("y", 4)]}
        slot_c = {2: [("x", 2, 0)], 4: [("x", 3, 0)]}
        pre = {2: [("ws", 1)], 4: [("ws", 2)], 6: [("ws", 3)]}
        post = {1: [("x", 1, 0), ("x", 1, 1)], 2: [("y", 0)], 3: [("x", 2, 0), ("x", 2, 1), ("y", 1)], 4: [("y", 2)], 5: [("x", 3, 0), ("x", 3, 1), ("y", 3)], 6: [("y", 4)], 7: [("y", 5)]}
        late_z = (2,4,6)
        for n in range(1, UNITS):
            for job in slot_a.get(n, []):
                turn_job(job)
            for i in range(3):
                discount_add(n - 1, i)
                if i == 0:
                    apply_gain(nc.gpsimd, gain, n - 1, 0)
                matmul_z(n, i + 1)
            apply_gain(nc.gpsimd, gain, n - 1, "pair")
            discount_add(n - 1, 3)
            round_y(n - 1, 0)
            for job in slot_b.get(n, []):
                turn_job(job)
            for c in range(4):
                hidden(n, c)
                if c == 0 and n + 1 < UNITS and n + 1 not in late_z:
                    matmul_z(n + 1, 0)
            for job in slot_c.get(n, []):
                turn_job(job)
            round_y(n - 1, "pair")
            apply_gain(nc.vector, gain_bank, n - 1, 3)
            round_y(n - 1, 3)
            for job in pre.get(n, []):
                quantize_job(job)
            hq[n] = quantize("h", 2, h_packed[n])
            for i in range(4):
                matmul_u(n, i)
            for job in post.get(n, []):
                quantize_job(job)
                if job[0] == "y" and job[1] % 2 == 1:
                    store_scales(nc.sync, job[1] // 2)
            if n + 1 in late_z:
                matmul_z(n + 1, 0)

        n = UNITS - 1
        turn_y(n - 1, 0, 2)
        turn_y(n - 1, 2, 4)
        discount_add(n, 0)
        apply_gain(nc.gpsimd, gain, n, 0)
        for i in range(1, 4):
            discount_add(n, i)
        round_y(n, 0)
        for i in range(1, 4):
            apply_gain(nc.vector, gain_bank, n, i)
            round_y(n, i)
        quantize_y(n - 1, 0, 4)
        turn_y(n, 0, 2, nc.vector.tensor_copy)
        turn_y(n, 2, 3)
        turn_y(n, 3, 4)
        quantize_y(n, 0, 2)
        quantize_y(n, 2, 3)
        quantize_y(n, 3, 4)
        store_scales(nc.scalar, B - 1)
